import numpy as np
import ml_dtypes


def mxq(x, axis, fmt="e4m3"):
    dtype, down = {"e4m3": (ml_dtypes.float8_e4m3fn, 7), "e5m2": (ml_dtypes.float8_e5m2, 14)}[fmt]
    v = np.moveaxis(np.asarray(x, np.float32).astype(ml_dtypes.bfloat16).astype(np.float64), axis, -1)
    blocks = v.reshape(v.shape[:-1] + (-1, 32))
    amax = np.abs(blocks).max(-1, keepdims=True)
    byte = np.maximum(np.where(amax > 0, np.frexp(amax)[1] - 1 + 127, 0) - down, 1)
    scale = np.exp2(byte - 127.0)
    codes = (blocks / scale).astype(np.float32).astype(dtype).astype(np.float64)
    return np.moveaxis((codes * scale).reshape(v.shape), -1, axis)


WIDE = False


def mx_kscale(k):
    if not WIDE:
        return np.ones(k)
    levels = np.array([10, -10, 5, -5, 0])
    if k % 512:
        return np.exp2(np.random.permutation(np.resize(levels, k // 32))).repeat(32)
    a = np.empty((k // 512, 16))
    for p in range(k // 512):
        a[p, :8] = np.random.permutation(np.resize(levels, 8))
        for g in range(8):
            far = levels[np.abs(levels - a[p, g]) >= 10]
            a[p, g + 8] = far[np.random.randint(len(far))]
    return np.exp2(a.ravel()).repeat(32)


def f64(x):
    return np.asarray(x).astype(np.float64)


def striped8(idx):
    return np.concatenate([v.reshape(-1, 16).T for v in idx]).astype(np.uint16)


def unstriped8(offs):
    return np.stack([offs[16 * g:16 * g + 16].T.reshape(-1) for g in range(8)]).astype(np.int64)


E2M1 = np.array([0.0, 0.5, 1.0, 1.5, 2.0, 3.0, 4.0, 6.0, -0.0, -0.5, -1.0, -1.5, -2.0, -3.0, -4.0, -6.0])


def pack_weight(w, fmt):
    k, n = w.shape
    w = f64(np.asarray(w, np.float32).astype(ml_dtypes.bfloat16)).reshape(k // 32, 32, n)
    amax = np.abs(w).max(1)
    if fmt == "e4m3":
        byte = np.frexp(amax)[1] - 1 + 127 - 7
    else:
        mant, ex = np.frexp(amax / 6.0)
        byte = np.where(mant > 0.5, ex, ex - 1) + 127
    byte = np.clip(np.where(amax > 0, byte, 1), 1, 254)
    scaled = (w * np.exp2(127.0 - byte)[:, None, :]).reshape(k, n).astype(np.float32)
    by_word = np.ascontiguousarray(scaled.reshape(k // 512, 128, 4, n).transpose(0, 1, 3, 2))
    if fmt == "e4m3":
        words = by_word.astype(ml_dtypes.float8_e4m3fn).view(np.uint8)
    else:
        c = by_word.astype(ml_dtypes.float4_e2m1fn).view(np.uint8) & 0xF
        words = (c[..., 0::2] | (c[..., 1::2] << 4)).reshape(k // 512, 128, 2 * n)
    return np.ascontiguousarray(words), np.ascontiguousarray(byte.astype(np.uint8).reshape(k // 512, 16, n))


def unpack_weight(words, scales, fmt):
    g, _, n = scales.shape
    words = np.ascontiguousarray(words).reshape(g, 128, n, -1)
    if fmt == "e4m3":
        vals = words.view(ml_dtypes.float8_e4m3fn).astype(np.float64)
    else:
        nib = np.empty((g, 128, n, 4), np.uint8)
        nib[..., 0::2] = words & 0xF
        nib[..., 1::2] = words >> 4
        vals = E2M1[nib]
    vals = vals * np.repeat(np.exp2(scales.astype(np.float64) - 127.0), 8, axis=1)[..., None]
    return vals.transpose(0, 1, 3, 2).reshape(g * 512, n)


K, M, T, S = 1024, 512, 1024, 512


def setup_inputs():
    n = np.random.standard_normal
    s = mx_kscale(K)[:, None]
    s2 = mx_kscale(512)[:, None]
    p_w4 = pack_weight(n((K, M)) / np.sqrt(K) / s, "e2m1")
    return {
        "xT": (n((K, T)) * s).astype(np.float32),
        "w4_words": p_w4[0],
        "w4_scales": p_w4[1],
        "c": (n((512, S)) * s2).astype(np.float32),
        "u": (n((512, M)) / np.sqrt(512) / s2).astype(np.float32),
        "wgt": np.repeat(np.random.uniform(0.5, 2.0, (8, S)), 16, axis=0).astype(np.float32),
        "b": (0.3 * n(512)).astype(np.float32),
        "wgo": np.repeat(np.random.uniform(0.5, 2.0, (8, S)), 16, axis=0).astype(np.float32),
        "offs": striped8(np.stack([np.random.permutation(T)[:S] for _ in range(8)])),
        "offs2": striped8(np.stack([np.random.permutation(T)[:S] for _ in range(8)])),
    }


def reference(xT, w4_words, w4_scales, c, u, wgt, b, wgo, offs, offs2):
    idx = unstriped8(offs)
    group = np.arange(K) % 512 // 64
    xg = f64(wgt)[np.arange(K) // 4 % 128] * f64(xT)[np.arange(K)[:, None], idx[group]]
    xT_ = mxq(xg, 0, "e4m3")
    w4_ = unpack_weight(w4_words, w4_scales, "e2m1")
    c_ = mxq(f64(c), 0, "e4m3")
    u_ = mxq(f64(u), 0, "e4m3")
    y = w4_.T @ xT_ + u_.T @ c_
    place = unstriped8(offs2)[np.arange(M) % 128 // 16]
    out = np.zeros((M, T))
    out[np.arange(M)[:, None], place] = f64(wgo)[np.arange(M) % 128] * (y + f64(b)[:, None])
    return out

@@ -1,0 +1,207 @@
+from contextlib import ExitStack
+
+import concourse.mybir as mybir
+from concourse.masks import make_identity
+
+K, M, T, S, L = 1024, 512, 1024, 512, 512
+FLOPS = 2 * (K + L) * M * S
+
+F32 = mybir.dt.float32
+BF16 = mybir.dt.bfloat16
+I32 = mybir.dt.int32
+U32 = mybir.dt.uint32
+U16 = mybir.dt.uint16
+U8 = mybir.dt.uint8
+FP8X4 = mybir.dt.float8_e4m3fn_x4
+FP4X4 = mybir.dt.float4_e2m1fn_x4
+MULT = mybir.AluOpType.mult
+IDENTITY = mybir.ActivationFunctionType.Identity
+
+P = 128
+PACK = 4
+GROUP = 16
+N_MM = 128
+SPANS = [(0, 128), (128, 256), (256, 512)]
+
+
+def tile_list_hboth_d_bias_kernel(tc, xT, w4_words, w4_scales, c, u, wgt, b, wgo, offs, offs2, out):
+    nc = tc.nc
+    with ExitStack() as ctx:
+        keep = ctx.enter_context(tc.tile_pool(name="keep", bufs=1))
+        psum = ctx.enter_context(tc.psum_pool(name="psum", bufs=7))
+        psum_b = ctx.enter_context(tc.psum_pool(name="psum_b", bufs=1))
+
+        def load(name, shape, dtype, src):
+            t = keep.tile(shape, dtype, name=name, align_bytes=64)
+            nc.sync.dma_start(out=t[:], in_=src)
+            return t
+
+        def interleave(dst, raw, engine=nc.scalar.copy):
+            engine(out=dst.rearrange("p (q r) i -> p q i r", r=4), in_=raw.rearrange("p i (q r) -> p q i r", r=4))
+
+        def staging(name, width):
+            return keep.tile([P, width, PACK], BF16, name=name, align_bytes=64)
+
+        def quantize(name, grouped):
+            width = grouped[:].shape[1]
+            codes = keep.tile([P, width], U32, name=name + "_codes", align_bytes=64)
+            scales = keep.tile([P, width], U8, name=name + "_scales", align_bytes=64)
+            nc.vector.quantize_mx(out=codes[:].bitcast(FP8X4), scales=scales[:], in_=grouped[:].rearrange("p w i -> p (w i)"))
+            return codes, scales
+
+        def part(q, lo, hi):
+            return q[0][:, lo:hi], q[1][:, lo:hi]
+
+        w_scales = keep.tile([P, 2 * M], U8, name="w_scales", align_bytes=64)
+        nc.vector.memset(w_scales[:].bitcast(U32), 0)
+        b_rows = keep.tile([P, P], F32, name="b_rows")
+        nc.vector.memset(b_rows[:], 0.0)
+        ident = keep.tile([P, P], F32, name="ident")
+        make_identity(nc, ident[:])
+        pages = [keep.tile([P, T], F32, name="page%d" % n) for n in range(4)]
+        for n in range(4):
+            (nc.vector if n < 2 else nc.gpsimd).memset(pages[n][:].bitcast(U32), 0)
+
+        offs_t = keep.tile([P, S // GROUP], U16, name="offs_t")
+        nc.sync.dma_start(offs_t[:], offs)
+        wgt_t = load("wgt_t", [P, S], F32, wgt)
+        x_planes = xT.rearrange("(a p i) t -> a i p t", a=2, i=PACK)
+        c_rows = c.rearrange("(p i) j -> p i j", i=PACK)
+        u_rows = u.rearrange("(p i) n -> p i n", i=PACK)
+        c_t, u_t = {}, {}
+        x_t = [[None] * PACK for a in range(2)]
+        for a in range(2):
+            for i in range(PACK):
+                if (a, i) == (1, 3):
+                    c_t[0] = load("c0", [P, PACK, 128], F32, c_rows[:, :, 0:128])
+                    u_t[0] = load("u0", [P, PACK, 128], F32, u_rows[:, :, 0:128])
+                x_t[a][i] = load("x%d%d" % (a, i), [P, T], F32, x_planes[a, i])
+                if (a, i) == (0, 1):
+                    for q in range(4):
+                        nc.sync.dma_start(
+                            out=w_scales[32 * q : 32 * q + 4, :].bitcast(I32).rearrange("r (a n) -> r a n", a=2),
+                            in_=w4_scales[:, 4 * q : 4 * q + 4, :].bitcast(I32).rearrange("a r n -> r a n"),
+                        )
+                    nc.sync.dma_start(out=b_rows[0:4, :], in_=b.rearrange("(m q) -> m q", q=P))
+        w_words = keep.tile([P, 2 * 2 * M], U8, name="w_words", align_bytes=64)
+        nc.sync.dma_start(
+            out=w_words[:].bitcast(I32).rearrange("p (a w) -> p a w", a=2),
+            in_=w4_words.bitcast(I32).rearrange("a p w -> p a w"),
+        )
+        offs2_t = keep.tile([P, S // GROUP], U16, name="offs2_t")
+        nc.sync.dma_start(offs2_t[:], offs2)
+        u_t[1] = load("u1", [P, PACK, 128], F32, u_rows[:, :, 128:256])
+        u_t[2] = load("u2", [P, PACK, 128], F32, u_rows[:, :, 256:384])
+        wgo_t = load("wgo_t", [P, S], F32, wgo)
+        u_t[3] = load("u3", [P, PACK, 128], F32, u_rows[:, :, 384:512])
+        c_t[1] = load("c1", [P, PACK, 128], F32, c_rows[:, :, 128:256])
+        c_t[2] = load("c2", [P, PACK, 256], F32, c_rows[:, :, 256:512])
+
+        b_ps = psum_b.tile([P, P], F32, name="b_ps")
+        nc.tensor.transpose(b_ps[:], b_rows[:], ident[:])
+        bias = keep.tile([P, 4], F32, name="bias")
+        nc.scalar.activation(out=bias[:], in_=b_ps[:, 0:4], func=IDENTITY)
+
+        def gather(dst, plane, j0, j1):
+            nc.vector.tensor_tensor(dst, plane[:].indirect(offs_t[:, j0 // GROUP : j1 // GROUP]), wgt_t[:, j0:j1], MULT)
+
+        early = staging("early", 256)
+        late = staging("late", 256)
+        xs1 = staging("xs1", 256)
+        xs2 = staging("xs2", 512)
+        g0 = keep.tile([P, PACK, S], F32, name="g0")
+        for i in range(PACK):
+            gather(g0[:, i, :], x_t[0][i], 0, S)
+        interleave(early[:, 0:128, :], g0[:, :, 0:128])
+        interleave(xs1[:, 0:128, :], g0[:, :, 128:256])
+        interleave(xs2[:, 0:256, :], g0[:, :, 256:512])
+        g1a = keep.tile([P, PACK, 128], F32, name="g1a")
+        g1b = keep.tile([P, PACK, 384], F32, name="g1b")
+        for i in range(PACK - 1):
+            gather(g1a[:, i, :], x_t[1][i], 0, 128)
+            gather(g1b[:, i, :], x_t[1][i], 128, S)
+        interleave(early[:, 128:256, :], c_t[0][:])
+        interleave(late[:, 0:128, :], u_t[0][:])
+        x0_q, x1_q, c_q, u_q = {}, {}, {}, {}
+        q = quantize("early", early)
+        x0_q[0], c_q[0] = part(q, 0, 128), part(q, 128, 256)
+        gather(g1a[:, 3, :], x_t[1][3], 0, 128)
+        interleave(late[:, 128:256, :], g1a[:])
+        gather(g1b[:, 3, :], x_t[1][3], 128, S)
+        q = quantize("late", late)
+        u_q[0], x1_q[0] = part(q, 0, 128), part(q, 128, 256)
+
+        def product(n, s):
+            j0, j1 = SPANS[s]
+            acc = psum.tile([P, j1 - j0], F32, name="acc")
+            for lo in range(0, j1 - j0, N_MM):
+                cols = slice(lo, lo + N_MM)
+                def w_pass(a, xq, start, stop):
+                    nc.tensor.matmul_mx(
+                        out=acc[:, cols],
+                        lhsT=w_words[:, 2 * (M * a + P * n) : 2 * (M * a + P * (n + 1))].bitcast(FP4X4),
+                        lhsT_scale=w_scales[:, M * a + P * n : M * a + P * (n + 1)],
+                        rhs=xq[0][:, cols].bitcast(FP8X4),
+                        rhs_scale=xq[1][:, cols],
+                        start=start,
+                        stop=stop,
+                    )
+                w_pass(0, x0_q[s], True, False)
+                w_pass(1, x1_q[s], False, False)
+                nc.tensor.matmul_mx(
+                    out=acc[:, cols],
+                    lhsT=u_q[n][0].bitcast(FP8X4),
+                    lhsT_scale=u_q[n][1],
+                    rhs=c_q[s][0][:, cols].bitcast(FP8X4),
+                    rhs_scale=c_q[s][1][:, cols],
+                    start=False,
+                    stop=True,
+                )
+            return acc
+
+        def finish(n, s):
+            j0, j1 = SPANS[s]
+            acc = product(n, s)
+            y = keep.tile([P, j1 - j0], F32, name="y%d%d" % (n, s))
+            nc.scalar.activation(out=y[:], in_=acc[:], func=IDENTITY, bias=bias[:, n : n + 1])
+            nc.vector.tensor_tensor(pages[n][:].indirect(offs2_t[:, j0 // GROUP : j1 // GROUP]), y[:], wgo_t[:, j0:j1], MULT)
+            if s == 2:
+                nc.sync.dma_start(out=out[P * n : P * (n + 1), :], in_=pages[n][:])
+
+        def prep_u(n, engine=nc.scalar.copy):
+            st = staging("u_bf%d" % n, 128)
+            interleave(st[:], u_t[n][:], engine)
+            u_q[n] = part(quantize("u%d" % n, st), 0, 128)
+
+        def prep_c(s):
+            w = SPANS[s][1] - SPANS[s][0]
+            st = staging("c_bf%d" % s, w)
+            for lo in range(0, w, 128):
+                interleave(st[:, lo : lo + 128, :], c_t[s][:, :, lo : lo + 128])
+            c_q[s] = part(quantize("c%d" % s, st), 0, w)
+
+        def prep_x(s, st):
+            j0, j1 = SPANS[s]
+            w = j1 - j0
+            for lo in range(0, w, 128):
+                interleave(st[:, w + lo : w + lo + 128, :], g1b[:, :, j0 - 128 + lo : j0 + lo])
+            q = quantize("xs%d" % s, st)
+            x0_q[s], x1_q[s] = part(q, 0, w), part(q, w, 2 * w)
+
+        prep_u(1, nc.vector.tensor_copy)
+        prep_x(1, xs1)
+        prep_u(2)
+        finish(0, 0)
+        prep_u(3)
+        finish(1, 0)
+        prep_c(1)
+        finish(2, 0)
+        finish(3, 0)
+        prep_x(2, xs2)
+        finish(0, 1)
+        finish(1, 1)
+        prep_c(2)
+        finish(2, 1)
+        finish(3, 1)
+        for n in range(4):
+            finish(n, 2)

@@ -53,18 +53,21 @@ def tile_list_hboth_d_bias_kernel(tc, xT, w4_words, w4_scales, c, u, wgt, b, wgo
             return q[0][:, lo:hi], q[1][:, lo:hi]
 
         w_scales = keep.tile([P, 2 * M], U8, name="w_scales", align_bytes=64)
-        nc.vector.memset(w_scales[:].bitcast(U32), 0)
         b_rows = keep.tile([P, P], F32, name="b_rows")
-        nc.vector.memset(b_rows[:], 0.0)
+        nc.gpsimd.memset(b_rows[:], 0.0)
+        nc.gpsimd.memset(w_scales[:].bitcast(U32), 0)
+        nc.gpsimd.dma_start(out=b_rows[0:4, :], in_=b.rearrange("(m q) -> m q", q=P))
+        for q in range(4):
+            nc.gpsimd.dma_start(
+                out=w_scales[32 * q : 32 * q + 4, :].bitcast(I32).rearrange("r (a n) -> r a n", a=2),
+                in_=w4_scales[:, 4 * q : 4 * q + 4, :].bitcast(I32).rearrange("a r n -> r a n"),
+            )
         ident = keep.tile([P, P], F32, name="ident")
         make_identity(nc, ident[:])
         pages = [keep.tile([P, T], F32, name="page%d" % n) for n in range(4)]
         for n in range(4):
-            (nc.vector if n < 2 else nc.gpsimd).memset(pages[n][:].bitcast(U32), 0)
+            (nc.vector if n < 3 else nc.gpsimd).memset(pages[n][:].bitcast(U32), 0)
 
-        offs_t = keep.tile([P, S // GROUP], U16, name="offs_t")
-        nc.sync.dma_start(offs_t[:], offs)
-        wgt_t = load("wgt_t", [P, S], F32, wgt)
         x_planes = xT.rearrange("(a p i) t -> a i p t", a=2, i=PACK)
         c_rows = c.rearrange("(p i) j -> p i j", i=PACK)
         u_rows = u.rearrange("(p i) n -> p i n", i=PACK)
@@ -76,13 +79,10 @@ def tile_list_hboth_d_bias_kernel(tc, xT, w4_words, w4_scales, c, u, wgt, b, wgo
                     c_t[0] = load("c0", [P, PACK, 128], F32, c_rows[:, :, 0:128])
                     u_t[0] = load("u0", [P, PACK, 128], F32, u_rows[:, :, 0:128])
                 x_t[a][i] = load("x%d%d" % (a, i), [P, T], F32, x_planes[a, i])
-                if (a, i) == (0, 1):
-                    for q in range(4):
-                        nc.sync.dma_start(
-                            out=w_scales[32 * q : 32 * q + 4, :].bitcast(I32).rearrange("r (a n) -> r a n", a=2),
-                            in_=w4_scales[:, 4 * q : 4 * q + 4, :].bitcast(I32).rearrange("a r n -> r a n"),
-                        )
-                    nc.sync.dma_start(out=b_rows[0:4, :], in_=b.rearrange("(m q) -> m q", q=P))
+                if (a, i) == (0, 0):
+                    wgt_t = load("wgt_t", [P, S], F32, wgt)
+                    offs_t = keep.tile([P, S // GROUP], U16, name="offs_t")
+                    nc.sync.dma_start(offs_t[:], offs)
         w_words = keep.tile([P, 2 * 2 * M], U8, name="w_words", align_bytes=64)
         nc.sync.dma_start(
             out=w_words[:].bitcast(I32).rearrange("p (a w) -> p a w", a=2),
@@ -92,8 +92,8 @@ def tile_list_hboth_d_bias_kernel(tc, xT, w4_words, w4_scales, c, u, wgt, b, wgo
         nc.sync.dma_start(offs2_t[:], offs2)
         u_t[1] = load("u1", [P, PACK, 128], F32, u_rows[:, :, 128:256])
         u_t[2] = load("u2", [P, PACK, 128], F32, u_rows[:, :, 256:384])
-        wgo_t = load("wgo_t", [P, S], F32, wgo)
         u_t[3] = load("u3", [P, PACK, 128], F32, u_rows[:, :, 384:512])
+        wgo_t = load("wgo_t", [P, S], F32, wgo)
         c_t[1] = load("c1", [P, PACK, 128], F32, c_rows[:, :, 128:256])
         c_t[2] = load("c2", [P, PACK, 256], F32, c_rows[:, :, 256:512])
 
@@ -115,19 +115,17 @@ def tile_list_hboth_d_bias_kernel(tc, xT, w4_words, w4_scales, c, u, wgt, b, wgo
         interleave(early[:, 0:128, :], g0[:, :, 0:128])
         interleave(xs1[:, 0:128, :], g0[:, :, 128:256])
         interleave(xs2[:, 0:256, :], g0[:, :, 256:512])
-        g1a = keep.tile([P, PACK, 128], F32, name="g1a")
-        g1b = keep.tile([P, PACK, 384], F32, name="g1b")
+        g1 = keep.tile([P, PACK, S], F32, name="g1")
         for i in range(PACK - 1):
-            gather(g1a[:, i, :], x_t[1][i], 0, 128)
-            gather(g1b[:, i, :], x_t[1][i], 128, S)
+            gather(g1[:, i, :], x_t[1][i], 0, S)
         interleave(early[:, 128:256, :], c_t[0][:])
         interleave(late[:, 0:128, :], u_t[0][:])
         x0_q, x1_q, c_q, u_q = {}, {}, {}, {}
         q = quantize("early", early)
         x0_q[0], c_q[0] = part(q, 0, 128), part(q, 128, 256)
-        gather(g1a[:, 3, :], x_t[1][3], 0, 128)
-        interleave(late[:, 128:256, :], g1a[:])
-        gather(g1b[:, 3, :], x_t[1][3], 128, S)
+        gather(g1[:, 3, 0:128], x_t[1][3], 0, 128)
+        interleave(late[:, 128:256, :], g1[:, :, 0:128])
+        gather(g1[:, 3, 128:S], x_t[1][3], 128, S)
         q = quantize("late", late)
         u_q[0], x1_q[0] = part(q, 0, 128), part(q, 128, 256)
 
@@ -184,7 +182,7 @@ def tile_list_hboth_d_bias_kernel(tc, xT, w4_words, w4_scales, c, u, wgt, b, wgo
             j0, j1 = SPANS[s]
             w = j1 - j0
             for lo in range(0, w, 128):
-                interleave(st[:, w + lo : w + lo + 128, :], g1b[:, :, j0 - 128 + lo : j0 + lo])
+                interleave(st[:, w + lo : w + lo + 128, :], g1[:, :, j0 + lo : j0 + lo + 128])
             q = quantize("xs%d" % s, st)
             x0_q[s], x1_q[s] = part(q, 0, w), part(q, w, 2 * w)
 
@@ -196,11 +194,17 @@ def tile_list_hboth_d_bias_kernel(tc, xT, w4_words, w4_scales, c, u, wgt, b, wgo
         finish(1, 0)
         prep_c(1)
         finish(2, 0)
+        interleave(xs2[:, 256:384, :], g1[:, :, 256:384])
         finish(3, 0)
-        prep_x(2, xs2)
+        interleave(xs2[:, 384:512, :], g1[:, :, 384:512])
+        q = quantize("xs2", xs2)
+        x0_q[2], x1_q[2] = part(q, 0, 256), part(q, 256, 512)
         finish(0, 1)
+        cs2 = staging("cs2", 256)
+        interleave(cs2[:, 0:128, :], c_t[2][:, :, 0:128])
         finish(1, 1)
-        prep_c(2)
+        interleave(cs2[:, 128:256, :], c_t[2][:, :, 128:256])
+        c_q[2] = part(quantize("c2", cs2), 0, 256)
         finish(2, 1)
         finish(3, 1)
         for n in range(4):

@@ -21,7 +21,6 @@ P = 128
 PACK = 4
 GROUP = 16
 N_MM = 128
-SPANS = [(0, 128), (128, 256), (256, 512)]
 
 
 def tile_list_hboth_d_bias_kernel(tc, xT, w4_words, w4_scales, c, u, wgt, b, wgo, offs, offs2, out):
@@ -32,7 +31,7 @@ def tile_list_hboth_d_bias_kernel(tc, xT, w4_words, w4_scales, c, u, wgt, b, wgo
         psum_b = ctx.enter_context(tc.psum_pool(name="psum_b", bufs=1))
 
         def load(name, shape, dtype, src):
-            t = keep.tile(shape, dtype, name=name, align_bytes=64)
+            t = keep.tile(shape, dtype, name=name, tag=name, align_bytes=64)
             nc.sync.dma_start(out=t[:], in_=src)
             return t
 
@@ -47,10 +46,7 @@ def tile_list_hboth_d_bias_kernel(tc, xT, w4_words, w4_scales, c, u, wgt, b, wgo
             codes = keep.tile([P, width], U32, name=name + "_codes", align_bytes=64)
             scales = keep.tile([P, width], U8, name=name + "_scales", align_bytes=64)
             nc.vector.quantize_mx(out=codes[:].bitcast(FP8X4), scales=scales[:], in_=grouped[:].rearrange("p w i -> p (w i)"))
-            return codes, scales
-
-        def part(q, lo, hi):
-            return q[0][:, lo:hi], q[1][:, lo:hi]
+            return [(codes[:, lo : lo + P], scales[:, lo : lo + P]) for lo in range(0, width, P)]
 
         w_scales = keep.tile([P, 2 * M], U8, name="w_scales", align_bytes=64)
         b_rows = keep.tile([P, P], F32, name="b_rows")
@@ -71,18 +67,20 @@ def tile_list_hboth_d_bias_kernel(tc, xT, w4_words, w4_scales, c, u, wgt, b, wgo
         x_planes = xT.rearrange("(a p i) t -> a i p t", a=2, i=PACK)
         c_rows = c.rearrange("(p i) j -> p i j", i=PACK)
         u_rows = u.rearrange("(p i) n -> p i n", i=PACK)
-        c_t, u_t = {}, {}
         x_t = [[None] * PACK for a in range(2)]
         for a in range(2):
             for i in range(PACK):
-                if (a, i) == (1, 3):
-                    c_t[0] = load("c0", [P, PACK, 128], F32, c_rows[:, :, 0:128])
-                    u_t[0] = load("u0", [P, PACK, 128], F32, u_rows[:, :, 0:128])
                 x_t[a][i] = load("x%d%d" % (a, i), [P, T], F32, x_planes[a, i])
                 if (a, i) == (0, 0):
                     wgt_t = load("wgt_t", [P, S], F32, wgt)
                     offs_t = keep.tile([P, S // GROUP], U16, name="offs_t")
                     nc.sync.dma_start(offs_t[:], offs)
+
+        def load_cols(name, rows, lo, hi):
+            return load(name, [P, PACK, hi - lo], F32, rows[:, :, lo:hi])
+
+        u0 = load_cols("u0", u_rows, 0, 128)
+        c0 = load_cols("c0", c_rows, 0, 128)
         w_words = keep.tile([P, 2 * 2 * M], U8, name="w_words", align_bytes=64)
         nc.sync.dma_start(
             out=w_words[:].bitcast(I32).rearrange("p (a w) -> p a w", a=2),
@@ -90,12 +88,13 @@ def tile_list_hboth_d_bias_kernel(tc, xT, w4_words, w4_scales, c, u, wgt, b, wgo
         )
         offs2_t = keep.tile([P, S // GROUP], U16, name="offs2_t")
         nc.sync.dma_start(offs2_t[:], offs2)
-        u_t[1] = load("u1", [P, PACK, 128], F32, u_rows[:, :, 128:256])
-        u_t[2] = load("u2", [P, PACK, 128], F32, u_rows[:, :, 256:384])
-        u_t[3] = load("u3", [P, PACK, 128], F32, u_rows[:, :, 384:512])
-        wgo_t = load("wgo_t", [P, S], F32, wgo)
-        c_t[1] = load("c1", [P, PACK, 128], F32, c_rows[:, :, 128:256])
-        c_t[2] = load("c2", [P, PACK, 256], F32, c_rows[:, :, 256:512])
+        u1 = load_cols("u1", u_rows, 128, 256)
+        c1 = load_cols("c1", c_rows, 128, 256)
+        wgo_lo = load("wgo_lo", [P, 256], F32, wgo[:, 0:256])
+        u2 = load_cols("u2", u_rows, 256, 384)
+        u3 = load_cols("u3", u_rows, 384, 512)
+        wgo_hi = load("wgo_hi", [P, 256], F32, wgo[:, 256:512])
+        c23 = load_cols("c23", c_rows, 256, 512)
 
         b_ps = psum_b.tile([P, P], F32, name="b_ps")
         nc.tensor.transpose(b_ps[:], b_rows[:], ident[:])
@@ -105,107 +104,82 @@ def tile_list_hboth_d_bias_kernel(tc, xT, w4_words, w4_scales, c, u, wgt, b, wgo
         def gather(dst, plane, j0, j1):
             nc.vector.tensor_tensor(dst, plane[:].indirect(offs_t[:, j0 // GROUP : j1 // GROUP]), wgt_t[:, j0:j1], MULT)
 
-        early = staging("early", 256)
-        late = staging("late", 256)
-        xs1 = staging("xs1", 256)
-        xs2 = staging("xs2", 512)
-        g0 = keep.tile([P, PACK, S], F32, name="g0")
-        for i in range(PACK):
-            gather(g0[:, i, :], x_t[0][i], 0, S)
-        interleave(early[:, 0:128, :], g0[:, :, 0:128])
-        interleave(xs1[:, 0:128, :], g0[:, :, 128:256])
-        interleave(xs2[:, 0:256, :], g0[:, :, 256:512])
-        g1 = keep.tile([P, PACK, S], F32, name="g1")
-        for i in range(PACK - 1):
-            gather(g1[:, i, :], x_t[1][i], 0, S)
-        interleave(early[:, 128:256, :], c_t[0][:])
-        interleave(late[:, 0:128, :], u_t[0][:])
         x0_q, x1_q, c_q, u_q = {}, {}, {}, {}
-        q = quantize("early", early)
-        x0_q[0], c_q[0] = part(q, 0, 128), part(q, 128, 256)
-        gather(g1[:, 3, 0:128], x_t[1][3], 0, 128)
-        interleave(late[:, 128:256, :], g1[:, :, 0:128])
-        gather(g1[:, 3, 128:S], x_t[1][3], 128, S)
-        q = quantize("late", late)
-        u_q[0], x1_q[0] = part(q, 0, 128), part(q, 128, 256)
 
-        def product(n, s):
-            j0, j1 = SPANS[s]
+        def finish(n, chunks, slot=None):
+            j0, j1 = P * chunks[0], P * (chunks[-1] + 1)
             acc = psum.tile([P, j1 - j0], F32, name="acc")
-            for lo in range(0, j1 - j0, N_MM):
-                cols = slice(lo, lo + N_MM)
-                def w_pass(a, xq, start, stop):
+            for j in chunks:
+                cols = slice(P * j - j0, P * (j + 1) - j0)
+                for a, xq in enumerate([x0_q[j], x1_q[j]]):
                     nc.tensor.matmul_mx(
                         out=acc[:, cols],
                         lhsT=w_words[:, 2 * (M * a + P * n) : 2 * (M * a + P * (n + 1))].bitcast(FP4X4),
                         lhsT_scale=w_scales[:, M * a + P * n : M * a + P * (n + 1)],
-                        rhs=xq[0][:, cols].bitcast(FP8X4),
-                        rhs_scale=xq[1][:, cols],
-                        start=start,
-                        stop=stop,
+                        rhs=xq[0].bitcast(FP8X4),
+                        rhs_scale=xq[1],
+                        start=(a == 0),
+                        stop=False,
                     )
-                w_pass(0, x0_q[s], True, False)
-                w_pass(1, x1_q[s], False, False)
                 nc.tensor.matmul_mx(
                     out=acc[:, cols],
                     lhsT=u_q[n][0].bitcast(FP8X4),
                     lhsT_scale=u_q[n][1],
-                    rhs=c_q[s][0][:, cols].bitcast(FP8X4),
-                    rhs_scale=c_q[s][1][:, cols],
+                    rhs=c_q[j][0].bitcast(FP8X4),
+                    rhs_scale=c_q[j][1],
                     start=False,
                     stop=True,
                 )
-            return acc
-
-        def finish(n, s):
-            j0, j1 = SPANS[s]
-            acc = product(n, s)
-            y = keep.tile([P, j1 - j0], F32, name="y%d%d" % (n, s))
+            y = keep.tile([P, j1 - j0], F32, name="y%d%d" % (n, chunks[0]), tag=slot or "y%d%d" % (n, chunks[0]), align_bytes=64)
             nc.scalar.activation(out=y[:], in_=acc[:], func=IDENTITY, bias=bias[:, n : n + 1])
-            nc.vector.tensor_tensor(pages[n][:].indirect(offs2_t[:, j0 // GROUP : j1 // GROUP]), y[:], wgo_t[:, j0:j1], MULT)
-            if s == 2:
+            weights = wgo_lo[:, j0:j1] if j0 < 256 else wgo_hi[:, j0 - 256 : j1 - 256]
+            nc.vector.tensor_tensor(pages[n][:].indirect(offs2_t[:, j0 // GROUP : j1 // GROUP]), y[:], weights, MULT)
+            if j1 == S:
                 nc.sync.dma_start(out=out[P * n : P * (n + 1), :], in_=pages[n][:])
 
-        def prep_u(n, engine=nc.scalar.copy):
-            st = staging("u_bf%d" % n, 128)
-            interleave(st[:], u_t[n][:], engine)
-            u_q[n] = part(quantize("u%d" % n, st), 0, 128)
+        def prep(name, raw, engine=nc.scalar.copy):
+            st = staging(name + "_bf", P)
+            interleave(st[:], raw[:], engine)
+            return quantize(name, st)[0]
 
-        def prep_c(s):
-            w = SPANS[s][1] - SPANS[s][0]
-            st = staging("c_bf%d" % s, w)
-            for lo in range(0, w, 128):
-                interleave(st[:, lo : lo + 128, :], c_t[s][:, :, lo : lo + 128])
-            c_q[s] = part(quantize("c%d" % s, st), 0, w)
-
-        def prep_x(s, st):
-            j0, j1 = SPANS[s]
-            w = j1 - j0
-            for lo in range(0, w, 128):
-                interleave(st[:, w + lo : w + lo + 128, :], g1[:, :, j0 + lo : j0 + lo + 128])
-            q = quantize("xs%d" % s, st)
-            x0_q[s], x1_q[s] = part(q, 0, w), part(q, w, 2 * w)
-
-        prep_u(1, nc.vector.tensor_copy)
-        prep_x(1, xs1)
-        prep_u(2)
-        finish(0, 0)
-        prep_u(3)
-        finish(1, 0)
-        prep_c(1)
-        finish(2, 0)
-        interleave(xs2[:, 256:384, :], g1[:, :, 256:384])
-        finish(3, 0)
-        interleave(xs2[:, 384:512, :], g1[:, :, 384:512])
-        q = quantize("xs2", xs2)
-        x0_q[2], x1_q[2] = part(q, 0, 256), part(q, 256, 512)
-        finish(0, 1)
+        xs0 = staging("xs0", 256)
+        xs1 = staging("xs1", 256)
+        xs2 = staging("xs2", 512)
+        uc0 = staging("uc0", 256)
         cs2 = staging("cs2", 256)
-        interleave(cs2[:, 0:128, :], c_t[2][:, :, 0:128])
-        finish(1, 1)
-        interleave(cs2[:, 128:256, :], c_t[2][:, :, 128:256])
-        c_q[2] = part(quantize("c2", cs2), 0, 256)
-        finish(2, 1)
-        finish(3, 1)
+        g0 = keep.tile([P, PACK, S], F32, name="g0")
+        g1 = keep.tile([P, PACK, S], F32, name="g1")
+        for i in range(PACK):
+            gather(g0[:, i, :], x_t[0][i], 0, S)
+        interleave(xs0[:, 0:128, :], g0[:, :, 0:128])
+        interleave(xs1[:, 0:128, :], g0[:, :, 128:256])
+        interleave(xs2[:, 0:256, :], g0[:, :, 256:512])
+        for i in range(PACK - 1):
+            gather(g1[:, i, :], x_t[1][i], 0, S)
+        gather(g1[:, 3, 0:128], x_t[1][3], 0, 128)
+        interleave(xs0[:, 128:256, :], g1[:, :, 0:128])
+        gather(g1[:, 3, 128:S], x_t[1][3], 128, S)
+        interleave(uc0[:, 0:128, :], u0[:])
+        interleave(uc0[:, 128:256, :], c0[:], nc.vector.tensor_copy)
+        x0_q[0], x1_q[0] = quantize("xs0", xs0)
+        u_q[0], c_q[0] = quantize("uc0", uc0)
+        interleave(xs1[:, 128:256, :], g1[:, :, 128:256])
+        u_q[1] = prep("u1", u1, nc.vector.tensor_copy)
+        x0_q[1], x1_q[1] = quantize("xs1", xs1)
+        interleave(xs2[:, 256:384, :], g1[:, :, 256:384])
+        finish(0, [0])
+        c_q[1] = prep("c1", c1)
+        finish(1, [0], "c1")
+        interleave(xs2[:, 384:512, :], g1[:, :, 384:512])
+        x0_q[2], x0_q[3], x1_q[2], x1_q[3] = quantize("xs2", xs2)
+        u_q[2] = prep("u2", u2)
+        finish(0, [1], "u2")
+        finish(1, [1])
+        u_q[3] = prep("u3", u3)
+        finish(2, [0, 1], "u3")
+        interleave(cs2[:, 0:128, :], c23[:, :, 0:128])
+        interleave(cs2[:, 128:256, :], c23[:, :, 128:256])
+        c_q[2], c_q[3] = quantize("cs2", cs2)
+        finish(3, [0, 1], "c23")
         for n in range(4):
-            finish(n, 2)
+            finish(n, [2, 3])

@@ -48,18 +48,12 @@ def tile_list_hboth_d_bias_kernel(tc, xT, w4_words, w4_scales, c, u, wgt, b, wgo
             nc.vector.quantize_mx(out=codes[:].bitcast(FP8X4), scales=scales[:], in_=grouped[:].rearrange("p w i -> p (w i)"))
             return [(codes[:, lo : lo + P], scales[:, lo : lo + P]) for lo in range(0, width, P)]
 
-        w_scales = keep.tile([P, 2 * M], U8, name="w_scales", align_bytes=64)
-        b_rows = keep.tile([P, P], F32, name="b_rows")
-        nc.gpsimd.memset(b_rows[:], 0.0)
-        nc.gpsimd.memset(w_scales[:].bitcast(U32), 0)
-        nc.gpsimd.dma_start(out=b_rows[0:4, :], in_=b.rearrange("(m q) -> m q", q=P))
-        for q in range(4):
-            nc.gpsimd.dma_start(
-                out=w_scales[32 * q : 32 * q + 4, :].bitcast(I32).rearrange("r (a n) -> r a n", a=2),
-                in_=w4_scales[:, 4 * q : 4 * q + 4, :].bitcast(I32).rearrange("a r n -> r a n"),
-            )
         ident = keep.tile([P, P], F32, name="ident")
         make_identity(nc, ident[:])
+        b_rows = keep.tile([P, P], F32, name="b_rows")
+        nc.gpsimd.memset(b_rows[:], 0.0)
+        w_scales = keep.tile([P, 2 * M], U8, name="w_scales", align_bytes=64)
+        nc.gpsimd.memset(w_scales[:].bitcast(U32), 0)
         pages = [keep.tile([P, T], F32, name="page%d" % n) for n in range(4)]
         for n in range(4):
             (nc.vector if n < 3 else nc.gpsimd).memset(pages[n][:].bitcast(U32), 0)
@@ -68,29 +62,44 @@ def tile_list_hboth_d_bias_kernel(tc, xT, w4_words, w4_scales, c, u, wgt, b, wgo
         c_rows = c.rearrange("(p i) j -> p i j", i=PACK)
         u_rows = u.rearrange("(p i) n -> p i n", i=PACK)
         x_t = [[None] * PACK for a in range(2)]
-        for a in range(2):
-            for i in range(PACK):
-                x_t[a][i] = load("x%d%d" % (a, i), [P, T], F32, x_planes[a, i])
-                if (a, i) == (0, 0):
-                    wgt_t = load("wgt_t", [P, S], F32, wgt)
-                    offs_t = keep.tile([P, S // GROUP], U16, name="offs_t")
-                    nc.sync.dma_start(offs_t[:], offs)
+
+        def load_scale_rows(q):
+            nc.sync.dma_start(
+                out=w_scales[32 * q : 32 * q + 4, :].bitcast(I32).rearrange("r (a n) -> r a n", a=2),
+                in_=w4_scales[:, 4 * q : 4 * q + 4, :].bitcast(I32).rearrange("a r n -> r a n"),
+            )
 
         def load_cols(name, rows, lo, hi):
             return load(name, [P, PACK, hi - lo], F32, rows[:, :, lo:hi])
 
+        x_t[0][0] = load("x00", [P, T], F32, x_planes[0, 0])
+        wgt_t = load("wgt_t", [P, S], F32, wgt)
+        offs_t = keep.tile([P, S // GROUP], U16, name="offs_t")
+        nc.sync.dma_start(offs_t[:], offs)
+        x_t[0][1] = load("x01", [P, T], F32, x_planes[0, 1])
+        nc.sync.dma_start(out=b_rows[0:4, :], in_=b.rearrange("(m q) -> m q", q=P))
+        x_t[0][2] = load("x02", [P, T], F32, x_planes[0, 2])
+        load_scale_rows(0)
+        x_t[0][3] = load("x03", [P, T], F32, x_planes[0, 3])
+        load_scale_rows(1)
+        x_t[1][0] = load("x10", [P, T], F32, x_planes[1, 0])
+        load_scale_rows(2)
+        x_t[1][1] = load("x11", [P, T], F32, x_planes[1, 1])
+        load_scale_rows(3)
+        x_t[1][2] = load("x12", [P, T], F32, x_planes[1, 2])
+        offs2_t = keep.tile([P, S // GROUP], U16, name="offs2_t")
+        nc.sync.dma_start(offs2_t[:], offs2)
         u0 = load_cols("u0", u_rows, 0, 128)
+        x_t[1][3] = load("x13", [P, T], F32, x_planes[1, 3])
         c0 = load_cols("c0", c_rows, 0, 128)
         w_words = keep.tile([P, 2 * 2 * M], U8, name="w_words", align_bytes=64)
         nc.sync.dma_start(
             out=w_words[:].bitcast(I32).rearrange("p (a w) -> p a w", a=2),
             in_=w4_words.bitcast(I32).rearrange("a p w -> p a w"),
         )
-        offs2_t = keep.tile([P, S // GROUP], U16, name="offs2_t")
-        nc.sync.dma_start(offs2_t[:], offs2)
         u1 = load_cols("u1", u_rows, 128, 256)
-        c1 = load_cols("c1", c_rows, 128, 256)
         wgo_lo = load("wgo_lo", [P, 256], F32, wgo[:, 0:256])
+        c1 = load_cols("c1", c_rows, 128, 256)
         u2 = load_cols("u2", u_rows, 256, 384)
         u3 = load_cols("u3", u_rows, 384, 512)
         wgo_hi = load("wgo_hi", [P, 256], F32, wgo[:, 256:512])
@@ -167,11 +176,11 @@ def tile_list_hboth_d_bias_kernel(tc, xT, w4_words, w4_scales, c, u, wgt, b, wgo
         u_q[1] = prep("u1", u1, nc.vector.tensor_copy)
         x0_q[1], x1_q[1] = quantize("xs1", xs1)
         interleave(xs2[:, 256:384, :], g1[:, :, 256:384])
+        interleave(xs2[:, 384:512, :], g1[:, :, 384:512])
+        x0_q[2], x0_q[3], x1_q[2], x1_q[3] = quantize("xs2", xs2)
         finish(0, [0])
         c_q[1] = prep("c1", c1)
         finish(1, [0], "c1")
-        interleave(xs2[:, 384:512, :], g1[:, :, 384:512])
-        x0_q[2], x0_q[3], x1_q[2], x1_q[3] = quantize("xs2", xs2)
         u_q[2] = prep("u2", u2)
         finish(0, [1], "u2")
         finish(1, [1])

from contextlib import ExitStack

import concourse.mybir as mybir
from concourse.masks import make_identity

K, M, T, S, L = 1024, 512, 1024, 512, 512
FLOPS = 2 * (K + L) * M * S

F32 = mybir.dt.float32
BF16 = mybir.dt.bfloat16
I32 = mybir.dt.int32
U32 = mybir.dt.uint32
U16 = mybir.dt.uint16
U8 = mybir.dt.uint8
FP8X4 = mybir.dt.float8_e4m3fn_x4
FP4X4 = mybir.dt.float4_e2m1fn_x4
MULT = mybir.AluOpType.mult
IDENTITY = mybir.ActivationFunctionType.Identity

P = 128
PACK = 4
GROUP = 16
N_MM = 128


def tile_list_hboth_d_bias_kernel(tc, xT, w4_words, w4_scales, c, u, wgt, b, wgo, offs, offs2, out):
    nc = tc.nc
    with ExitStack() as ctx:
        keep = ctx.enter_context(tc.tile_pool(name="keep", bufs=1))
        psum = ctx.enter_context(tc.psum_pool(name="psum", bufs=7))
        psum_b = ctx.enter_context(tc.psum_pool(name="psum_b", bufs=1))

        def load(name, shape, dtype, src):
            t = keep.tile(shape, dtype, name=name, tag=name, align_bytes=64)
            nc.sync.dma_start(out=t[:], in_=src)
            return t

        def interleave(dst, raw, engine=nc.scalar.copy):
            engine(out=dst.rearrange("p (q r) i -> p q i r", r=4), in_=raw.rearrange("p i (q r) -> p q i r", r=4))

        def staging(name, width):
            return keep.tile([P, width, PACK], BF16, name=name, align_bytes=64)

        def quantize(name, grouped):
            width = grouped[:].shape[1]
            codes = keep.tile([P, width], U32, name=name + "_codes", align_bytes=64)
            scales = keep.tile([P, width], U8, name=name + "_scales", align_bytes=64)
            nc.vector.quantize_mx(out=codes[:].bitcast(FP8X4), scales=scales[:], in_=grouped[:].rearrange("p w i -> p (w i)"))
            return [(codes[:, lo : lo + P], scales[:, lo : lo + P]) for lo in range(0, width, P)]

        ident = keep.tile([P, P], F32, name="ident")
        make_identity(nc, ident[:])
        b_rows = keep.tile([P, P], F32, name="b_rows")
        nc.gpsimd.memset(b_rows[:], 0.0)
        w_scales = keep.tile([P, 2 * M], U8, name="w_scales", align_bytes=64)
        nc.gpsimd.memset(w_scales[:].bitcast(U32), 0)
        pages = [keep.tile([P, T], F32, name="page%d" % n) for n in range(4)]
        for n in range(4):
            (nc.vector if n < 3 else nc.gpsimd).memset(pages[n][:].bitcast(U32), 0)

        x_planes = xT.rearrange("(a p i) t -> a i p t", a=2, i=PACK)
        c_rows = c.rearrange("(p i) j -> p i j", i=PACK)
        u_rows = u.rearrange("(p i) n -> p i n", i=PACK)
        x_t = [[None] * PACK for a in range(2)]

        def load_scale_rows(q):
            nc.sync.dma_start(
                out=w_scales[32 * q : 32 * q + 4, :].bitcast(I32).rearrange("r (a n) -> r a n", a=2),
                in_=w4_scales[:, 4 * q : 4 * q + 4, :].bitcast(I32).rearrange("a r n -> r a n"),
            )

        def load_cols(name, rows, lo, hi):
            return load(name, [P, PACK, hi - lo], F32, rows[:, :, lo:hi])

        x_t[0][0] = load("x00", [P, T], F32, x_planes[0, 0])
        wgt_t = load("wgt_t", [P, S], F32, wgt)
        offs_t = keep.tile([P, S // GROUP], U16, name="offs_t")
        nc.sync.dma_start(offs_t[:], offs)
        x_t[0][1] = load("x01", [P, T], F32, x_planes[0, 1])
        nc.sync.dma_start(out=b_rows[0:4, :], in_=b.rearrange("(m q) -> m q", q=P))
        x_t[0][2] = load("x02", [P, T], F32, x_planes[0, 2])
        load_scale_rows(0)
        x_t[0][3] = load("x03", [P, T], F32, x_planes[0, 3])
        load_scale_rows(1)
        x_t[1][0] = load("x10", [P, T], F32, x_planes[1, 0])
        load_scale_rows(2)
        x_t[1][1] = load("x11", [P, T], F32, x_planes[1, 1])
        load_scale_rows(3)
        x_t[1][2] = load("x12", [P, T], F32, x_planes[1, 2])
        offs2_t = keep.tile([P, S // GROUP], U16, name="offs2_t")
        nc.sync.dma_start(offs2_t[:], offs2)
        u0 = load_cols("u0", u_rows, 0, 128)
        x_t[1][3] = load("x13", [P, T], F32, x_planes[1, 3])
        c0 = load_cols("c0", c_rows, 0, 128)
        w_words = keep.tile([P, 2 * 2 * M], U8, name="w_words", align_bytes=64)
        nc.sync.dma_start(
            out=w_words[:].bitcast(I32).rearrange("p (a w) -> p a w", a=2),
            in_=w4_words.bitcast(I32).rearrange("a p w -> p a w"),
        )
        u1 = load_cols("u1", u_rows, 128, 256)
        wgo_lo = load("wgo_lo", [P, 256], F32, wgo[:, 0:256])
        c1 = load_cols("c1", c_rows, 128, 256)
        u2 = load_cols("u2", u_rows, 256, 384)
        u3 = load_cols("u3", u_rows, 384, 512)
        wgo_hi = load("wgo_hi", [P, 256], F32, wgo[:, 256:512])
        c23 = load_cols("c23", c_rows, 256, 512)

        b_ps = psum_b.tile([P, P], F32, name="b_ps")
        nc.tensor.transpose(b_ps[:], b_rows[:], ident[:])
        bias = keep.tile([P, 4], F32, name="bias")
        nc.scalar.activation(out=bias[:], in_=b_ps[:, 0:4], func=IDENTITY)

        def gather(dst, plane, j0, j1):
            nc.vector.tensor_tensor(dst, plane[:].indirect(offs_t[:, j0 // GROUP : j1 // GROUP]), wgt_t[:, j0:j1], MULT)

        x0_q, x1_q, c_q, u_q = {}, {}, {}, {}

        def finish(n, chunks, slot=None):
            j0, j1 = P * chunks[0], P * (chunks[-1] + 1)
            acc = psum.tile([P, j1 - j0], F32, name="acc")
            for j in chunks:
                cols = slice(P * j - j0, P * (j + 1) - j0)
                for a, xq in enumerate([x0_q[j], x1_q[j]]):
                    nc.tensor.matmul_mx(
                        out=acc[:, cols],
                        lhsT=w_words[:, 2 * (M * a + P * n) : 2 * (M * a + P * (n + 1))].bitcast(FP4X4),
                        lhsT_scale=w_scales[:, M * a + P * n : M * a + P * (n + 1)],
                        rhs=xq[0].bitcast(FP8X4),
                        rhs_scale=xq[1],
                        start=(a == 0),
                        stop=False,
                    )
                nc.tensor.matmul_mx(
                    out=acc[:, cols],
                    lhsT=u_q[n][0].bitcast(FP8X4),
                    lhsT_scale=u_q[n][1],
                    rhs=c_q[j][0].bitcast(FP8X4),
                    rhs_scale=c_q[j][1],
                    start=False,
                    stop=True,
                )
            y = keep.tile([P, j1 - j0], F32, name="y%d%d" % (n, chunks[0]), tag=slot or "y%d%d" % (n, chunks[0]), align_bytes=64)
            nc.scalar.activation(out=y[:], in_=acc[:], func=IDENTITY, bias=bias[:, n : n + 1])
            weights = wgo_lo[:, j0:j1] if j0 < 256 else wgo_hi[:, j0 - 256 : j1 - 256]
            nc.vector.tensor_tensor(pages[n][:].indirect(offs2_t[:, j0 // GROUP : j1 // GROUP]), y[:], weights, MULT)
            if j1 == S:
                nc.sync.dma_start(out=out[P * n : P * (n + 1), :], in_=pages[n][:])

        def prep(name, raw, engine=nc.scalar.copy):
            st = staging(name + "_bf", P)
            interleave(st[:], raw[:], engine)
            return quantize(name, st)[0]

        xs0 = staging("xs0", 256)
        xs1 = staging("xs1", 256)
        xs2 = staging("xs2", 512)
        uc0 = staging("uc0", 256)
        cs2 = staging("cs2", 256)
        g0 = keep.tile([P, PACK, S], F32, name="g0")
        g1 = keep.tile([P, PACK, S], F32, name="g1")
        for i in range(PACK):
            gather(g0[:, i, :], x_t[0][i], 0, S)
        interleave(xs0[:, 0:128, :], g0[:, :, 0:128])
        interleave(xs1[:, 0:128, :], g0[:, :, 128:256])
        interleave(xs2[:, 0:256, :], g0[:, :, 256:512])
        for i in range(PACK - 1):
            gather(g1[:, i, :], x_t[1][i], 0, S)
        gather(g1[:, 3, 0:128], x_t[1][3], 0, 128)
        interleave(xs0[:, 128:256, :], g1[:, :, 0:128])
        gather(g1[:, 3, 128:S], x_t[1][3], 128, S)
        interleave(uc0[:, 0:128, :], u0[:])
        interleave(uc0[:, 128:256, :], c0[:], nc.vector.tensor_copy)
        x0_q[0], x1_q[0] = quantize("xs0", xs0)
        u_q[0], c_q[0] = quantize("uc0", uc0)
        interleave(xs1[:, 128:256, :], g1[:, :, 128:256])
        u_q[1] = prep("u1", u1, nc.vector.tensor_copy)
        x0_q[1], x1_q[1] = quantize("xs1", xs1)
        interleave(xs2[:, 256:384, :], g1[:, :, 256:384])
        interleave(xs2[:, 384:512, :], g1[:, :, 384:512])
        x0_q[2], x0_q[3], x1_q[2], x1_q[3] = quantize("xs2", xs2)
        finish(0, [0])
        c_q[1] = prep("c1", c1)
        finish(1, [0], "c1")
        u_q[2] = prep("u2", u2)
        finish(0, [1], "u2")
        finish(1, [1])
        u_q[3] = prep("u3", u3)
        finish(2, [0, 1], "u3")
        interleave(cs2[:, 0:128, :], c23[:, :, 0:128])
        interleave(cs2[:, 128:256, :], c23[:, :, 128:256])
        c_q[2], c_q[3] = quantize("cs2", cs2)
        finish(3, [0, 1], "c23")
        for n in range(4):
            finish(n, [2, 3])
